import numpy as np
import ml_dtypes


def mxq(x, axis, fmt="e4m3"):
    dtype, down = {"e4m3": (ml_dtypes.float8_e4m3fn, 7), "e5m2": (ml_dtypes.float8_e5m2, 14)}[fmt]
    v = np.moveaxis(np.asarray(x, np.float32).astype(ml_dtypes.bfloat16).astype(np.float64), axis, -1)
    blocks = v.reshape(v.shape[:-1] + (-1, 32))
    amax = np.abs(blocks).max(-1, keepdims=True)
    byte = np.maximum(np.where(amax > 0, np.frexp(amax)[1] - 1 + 127, 0) - down, 1)
    scale = np.exp2(byte - 127.0)
    codes = (blocks / scale).astype(np.float32).astype(dtype).astype(np.float64)
    return np.moveaxis((codes * scale).reshape(v.shape), -1, axis)


WIDE = False


def mx_kscale(k):
    if not WIDE:
        return np.ones(k)
    levels = np.array([10, -10, 5, -5, 0])
    if k % 512:
        return np.exp2(np.random.permutation(np.resize(levels, k // 32))).repeat(32)
    a = np.empty((k // 512, 16))
    for p in range(k // 512):
        a[p, :8] = np.random.permutation(np.resize(levels, 8))
        for g in range(8):
            far = levels[np.abs(levels - a[p, g]) >= 10]
            a[p, g + 8] = far[np.random.randint(len(far))]
    return np.exp2(a.ravel()).repeat(32)


BF16 = ml_dtypes.bfloat16


def bf(x):
    return np.asarray(x, np.float32).astype(BF16)


def f64(x):
    return np.asarray(x).astype(np.float64)


E2M1 = np.array([0.0, 0.5, 1.0, 1.5, 2.0, 3.0, 4.0, 6.0, -0.0, -0.5, -1.0, -1.5, -2.0, -3.0, -4.0, -6.0])


def pack_weight(w, fmt):
    k, n = w.shape
    w = f64(bf(w)).reshape(k // 32, 32, n)
    amax = np.abs(w).max(1)
    if fmt == "e4m3":
        byte = np.frexp(amax)[1] - 1 + 127 - 7
    else:
        mant, ex = np.frexp(amax / 6.0)
        byte = np.where(mant > 0.5, ex, ex - 1) + 127
    byte = np.clip(np.where(amax > 0, byte, 1), 1, 254)
    scaled = (w * np.exp2(127.0 - byte)[:, None, :]).reshape(k, n).astype(np.float32)
    by_word = np.ascontiguousarray(scaled.reshape(k // 512, 128, 4, n).transpose(0, 1, 3, 2))
    if fmt == "e4m3":
        words = by_word.astype(ml_dtypes.float8_e4m3fn).view(np.uint8)
    else:
        c = by_word.astype(ml_dtypes.float4_e2m1fn).view(np.uint8) & 0xF
        words = c[..., 0::2] | (c[..., 1::2] << 4)
    return np.ascontiguousarray(words), np.ascontiguousarray(byte.astype(np.uint8).reshape(k // 512, 16, n))


def unpack_weight(words, scales, fmt):
    g, p, n, _ = words.shape
    if fmt == "e4m3":
        vals = np.ascontiguousarray(words).view(ml_dtypes.float8_e4m3fn).astype(np.float64)
    else:
        nib = np.empty((g, p, n, 4), np.uint8)
        nib[..., 0::2] = words & 0xF
        nib[..., 1::2] = words >> 4
        vals = E2M1[nib]
    vals = vals * np.repeat(np.exp2(scales.astype(np.float64) - 127.0), 8, axis=1)[..., None]
    return vals.transpose(0, 1, 3, 2).reshape(g * 512, n)
def pack4(w):
    words, scales = pack_weight(w, "e2m1")
    return words.reshape(words.shape[0], 128, -1), scales


def unpack4(words, scales):
    return unpack_weight(words.reshape(words.shape[0], 128, -1, 2), scales, "e2m1")


G, S, R, M = 4, 768, 1024, 512


def setup_inputs():
    s = mx_kscale(G * R)
    t = mx_kscale(G * M)
    modes = np.random.standard_normal((G, R, M)) / np.sqrt(R)
    u_words, u_scales = pack4(modes.reshape(G * R, M) / s[:, None])
    v_words, v_scales = pack4(modes.transpose(0, 2, 1).reshape(G * M, R) / t[:, None])
    return {"probes": bf(np.random.standard_normal((G, S, R)) * s.reshape(G, 1, R)),
            "u_words": u_words, "u_scales": u_scales,
            "inv_lam": bf(np.exp(0.4 * np.random.standard_normal((G, M))) * t.reshape(G, M)),
            "v_words": v_words, "v_scales": v_scales,
            "inv_sd_probe": bf(np.exp(0.25 * np.random.standard_normal((G, S)))),
            "inv_sd_res": bf(np.exp(0.25 * np.random.standard_normal((G, R))))}


def reference(probes, u_words, u_scales, inv_lam, v_words, v_scales, inv_sd_probe, inv_sd_res):
    u = unpack4(u_words, u_scales).reshape(G, R, M)
    v = unpack4(v_words, v_scales).reshape(G, M, R)
    amp = mxq(f64(probes), 2, "e4m3") @ u
    h = amp * f64(inv_lam)[:, None, :]
    cov = mxq(h, 2, "e4m3") @ v
    return cov * f64(inv_sd_probe)[:, :, None] * f64(inv_sd_res)[:, None, :]

@@ -1,0 +1,327 @@
+from contextlib import ExitStack
+
+import concourse.mybir as mybir
+from concourse.masks import make_identity
+
+CFG = {"hq":[3,3,3,3,3,3,3,3,3,2,2,2],"kinds":"BAaAaBAaBAaB","loads":"lam x0 x1 U0 us0 P1 isr P2 gvs gusr V0 U1 isp P3 U2 P4 U3 P5 V1 P6 P7 P8 V2 P9 P10 P11 V3","j":[0,2,3,4,5,6,7,8,9,10,11,12],"s2":[1,3,4,5,6,7,8,9,10,11,12,13],"sort":[-9,-1,0,2],"plane":[-9,1,2,5],"late":[0]}
+G, S, R, M = 4, 768, 1024, 512
+FLOPS = 2 * 2 * G * S * R * M
+
+F32 = mybir.dt.float32
+BF16 = mybir.dt.bfloat16
+I32 = mybir.dt.int32
+U32 = mybir.dt.uint32
+U8 = mybir.dt.uint8
+FP8X4 = mybir.dt.float8_e4m3fn_x4
+FP4X4 = mybir.dt.float4_e2m1fn_x4
+COPY = mybir.ActivationFunctionType.Copy
+MULT = mybir.AluOpType.mult
+
+P = 128
+PACK = 4
+BANK = 512
+TILES = S // P
+PAIRS = TILES // 2
+PAIR = 2 * P
+PASSES = R // (P * PACK)
+STEPS = G * PAIRS
+KINDS = CFG.get("kinds", "AaB" * 4)
+T_STEP = CFG.get("t", [j - 2 for j in range(STEPS)])
+J_STEP = CFG.get("j", [j + 1 for j in range(STEPS)])
+S2_STEP = CFG.get("s2", [j + 2 for j in range(STEPS)])
+SORT_STEP = CFG.get("sort", [-9, -1, 0, 1])
+PLANE_STEP = CFG.get("plane", [-9, 1, 2, 3])
+HQ_AFTER = CFG.get("hq", [4] * STEPS)
+
+
+def tile_elastic_mode_correlation_s14_kernel(
+    tc, probes, u_words, u_scales, inv_lam, v_words, v_scales, inv_sd_probe, inv_sd_res, out
+):
+    nc = tc.nc
+    with ExitStack() as ctx:
+        keep = ctx.enter_context(tc.tile_pool(name="keep", bufs=1))
+        work = ctx.enter_context(tc.tile_pool(name="work", bufs=2))
+        psum = ctx.enter_context(tc.psum_pool(name="psum", bufs=2))
+        ctx.enter_context(tc.manual_schedule())
+
+        def kept(shape, dtype, name):
+            return keep.tile(shape, dtype, name=name, align_bytes=64)
+
+        ident = kept([P, P], F32, "ident")
+        make_identity(nc, ident[:])
+
+        us_first = kept([P, PASSES, M], U8, "us_first")
+        us_rest = kept([P, (G - 1) * PASSES, M], U8, "us_rest")
+        vs = kept([P, G, R], U8, "vs")
+        for plane in (us_first, vs, us_rest):
+            nc.vector.memset(plane[:].bitcast(I32), 0)
+
+        def load_scale_rows(queue, plane, rows):
+            for r in range(4):
+                queue.dma_start(
+                    out=plane[:].bitcast(I32)[r:P:32],
+                    in_=rows.bitcast(I32)[:, r:16:4, :].rearrange("g q n -> q g n"),
+                )
+
+        u_raw = [kept([P, PASSES, 2 * M], U8, "u_raw%d" % d) for d in range(G)]
+        v_raw = [kept([P, 2 * R], U8, "v_raw%d" % d) for d in range(G)]
+        x_rows = [kept([P, R], BF16, "x%d" % i) for i in range(2)]
+        x_pair = [None] + [kept([P, 2, R], BF16, "xp%d" % j) for j in range(1, STEPS)]
+        lam_bf = kept([P, G, PACK], BF16, "lam_bf")
+        lam = kept([P, G, PACK], F32, "lam")
+        isp = kept([P, G, TILES], BF16, "isp")
+        isr_rows = kept([P, G, R // P], BF16, "isr_rows")
+
+        x_hbm = probes.rearrange("d (p j) r -> d p j r", j=TILES)
+        out_hbm = out.rearrange("d (p j) r -> d p j r", j=TILES)
+
+        def load_u(d):
+            nc.sync.dma_start(
+                out=u_raw[d][:].bitcast(I32),
+                in_=u_words.bitcast(I32)[PASSES * d : PASSES * (d + 1)].rearrange("g p n -> p g n"),
+            )
+
+        def load_v(d):
+            nc.sync.dma_start(out=v_raw[d][:].bitcast(I32), in_=v_words.bitcast(I32)[d])
+
+        def load_pair(j):
+            d, i = divmod(j, PAIRS)
+            nc.sync.dma_start(out=x_pair[j][:], in_=x_hbm[d, :, 2 * i : 2 * i + 2, :])
+
+        def small(name):
+            if name == "lam":
+                nc.sync.dma_start(out=lam_bf[:], in_=inv_lam.rearrange("d (p t) -> p d t", t=PACK))
+            if name == "isr":
+                nc.sync.dma_start(out=isr_rows[:], in_=inv_sd_res.rearrange("d (p c) -> p d c", p=P))
+            if name == "isp":
+                nc.sync.dma_start(out=isp[:], in_=inv_sd_probe.rearrange("d (p j) -> p d j", j=TILES))
+            if name == "us0":
+                load_scale_rows(nc.sync, us_first, u_scales[0:PASSES])
+            if name == "usr":
+                load_scale_rows(nc.sync, us_rest, u_scales[PASSES:])
+            if name == "vs":
+                load_scale_rows(nc.sync, vs, v_scales)
+            if name == "gusr":
+                load_scale_rows(nc.gpsimd, us_rest, u_scales[PASSES:])
+            if name == "gvs":
+                load_scale_rows(nc.gpsimd, vs, v_scales)
+            if name == "gus0":
+                load_scale_rows(nc.gpsimd, us_first, u_scales[0:PASSES])
+            if name[0] == "x":
+                a = int(name[1:])
+                nc.sync.dma_start(out=x_rows[a][:], in_=x_hbm[0, :, a, :])
+            if name[0] == "P":
+                load_pair(int(name[1:]))
+            if name[0] == "U":
+                load_u(int(name[1:]))
+            if name[0] == "V":
+                load_v(int(name[1:]))
+
+        for name in CFG.get("loads", "isr x0 x1 U0 us0 lam P1 gvs gusr P2 U1 V0 isp P3 U2 P4 U3 P5 V1 P6 P7 P8 V2 P9 P10 P11 V3").split():
+            small(name)
+
+        nc.scalar.activation(out=lam[:], in_=lam_bf[:], func=COPY)
+
+        u_codes = [kept([P, PASSES, PACK, 2 * P], U8, "u_codes%d" % d) for d in range(G)]
+        u_plane = [kept([P, PASSES, PACK, P], U8, "u_plane%d" % d) for d in range(G)]
+        isr = [kept([P, R], BF16, "isr%d" % d) for d in range(G)]
+
+        def sort_u(d):
+            nc.vector.tensor_copy(
+                out=u_codes[d][:].rearrange("p g t (m b) -> p g t m b", b=2),
+                in_=u_raw[d][:].rearrange("p g (m t b) -> p g t m b", t=PACK, b=2),
+            )
+
+        def sort_plane(d):
+            rows = us_first[:] if d == 0 else us_rest[:, PASSES * (d - 1) : PASSES * d, :]
+            nc.vector.tensor_copy(out=u_plane[d][:], in_=rows.rearrange("p g (m t) -> p g t m", t=PACK))
+
+        def spread_isr(d):
+            bank = psum.tile([P, BANK], F32, name="spread", tag="cov", bufs=4)
+            words = isr_rows[:].bitcast(F32)
+            for c in range(4):
+                nc.tensor.transpose(
+                    bank[:, c * P : (c + 1) * P], words[:, d, c : c + 1].to_broadcast([P, P]), ident[:]
+                )
+            nc.scalar.copy(
+                out=isr[d][:].bitcast(F32).rearrange("p (q c) -> p q c", c=4),
+                in_=bank[:].rearrange("p (c q) -> p q c", c=4),
+            )
+
+        x_quad, x_codes, x_plane, amp, h_half, h_quad, h_codes, h_plane, cov = {}, {}, {}, {}, {}, {}, {}, {}, {}
+
+        def turn_probes(j):
+            x_quad[j] = work.tile([P, PASSES, PAIR, PACK], BF16, name="x_quad", align_bytes=64, bufs=3)
+            for a in range(2):
+                rows = x_rows[a][:] if j == 0 else x_pair[j][:, a, :]
+                words = rows.bitcast(F32)
+                bank = psum.tile([P, BANK], F32, name="turned", tag="turned")
+                for g in range(PASSES):
+                    for u in range(2):
+                        c = 2 * g + u
+                        nc.tensor.transpose(
+                            bank[:, c * P : (c + 1) * P], words[:, 256 * g + u : 256 * (g + 1) : 2], ident[:]
+                        )
+                nc.scalar.copy(
+                    out=x_quad[j][:].bitcast(F32)[:, :, a * P : (a + 1) * P, :],
+                    in_=bank[:].rearrange("p (g u r) -> p g r u", g=PASSES, u=2),
+                )
+
+        def quantize_probes(j):
+            d, i = divmod(j, PAIRS)
+            chunk = j - (KINDS[j] == "a")
+            if KINDS[j] != "a":
+                x_codes[chunk] = work.tile([P, PASSES, BANK], U32, name="x_codes", align_bytes=64, bufs=3)
+                x_plane[chunk] = work.tile([P, PASSES, BANK], U8, name="x_plane", align_bytes=64, bufs=3)
+            cols = slice(PAIR, 2 * PAIR) if KINDS[j] == "a" else slice(0, PAIR)
+            for g in range(PASSES):
+                nc.vector.quantize_mx(
+                    out=x_codes[chunk][:, g, cols].bitcast(FP8X4),
+                    scales=x_plane[chunk][:, g, cols],
+                    in_=x_quad[j][:, g].rearrange("p n t -> p (n t)"),
+                )
+
+        def project(bank_cols, d, t, chunk, cols):
+            for g in range(PASSES):
+                nc.tensor.matmul_mx(
+                    out=bank_cols,
+                    lhsT=u_codes[d][:, g, t, :].bitcast(FP4X4),
+                    lhsT_scale=u_plane[d][:, g, t, :],
+                    rhs=x_codes[chunk][:, g, cols].bitcast(FP8X4),
+                    rhs_scale=x_plane[chunk][:, g, cols],
+                    start=(g == 0),
+                    stop=(g == PASSES - 1),
+                )
+
+        def stage_one(j):
+            d, i = divmod(j, PAIRS)
+            chunk = j - (KINDS[j] == "a")
+            amp[j] = []
+            for b in range(2):
+                bank = psum.tile([P, BANK], F32, name="amp", tag="amp")
+                if KINDS[j] != "B":
+                    i = int(KINDS[j] == "a")
+                    project(bank[:], d, 2 * b + i, chunk, slice(0, BANK))
+                    amp[j].append((2 * b + i, bank[:], BANK))
+                else:
+                    for e in range(2):
+                        for a in range(2):
+                            c = 2 * e + a
+                            project(bank[:, c * P : (c + 1) * P], d, 2 * e + b, chunk, slice(a * P, (a + 1) * P))
+                        amp[j].append((2 * e + b, bank[:, e * PAIR : (e + 1) * PAIR], PAIR))
+
+        def scale_amplitudes(j):
+            d, i = divmod(j, PAIRS)
+            chunk = j - (KINDS[j] == "a")
+            if KINDS[j] != "a":
+                h_half[chunk] = work.tile([P, 2, BANK, 2], BF16, name="h_half", bufs=3)
+            for t, bank_cols, width in amp[j]:
+                nc.scalar.activation(
+                    out=h_half[chunk][:, t // 2, 0:width, t % 2],
+                    in_=bank_cols,
+                    func=COPY,
+                    scale=lam[:, d, t : t + 1],
+                )
+
+        def join_halves(j):
+            d, i = divmod(j, PAIRS)
+            cols = slice(PAIR, 2 * PAIR) if KINDS[j] == "a" else slice(0, PAIR)
+            h_quad[j] = work.tile([P, PAIR, PACK], BF16, name="h_quad", align_bytes=64, bufs=3)
+            nc.scalar.copy(
+                out=h_quad[j][:].bitcast(F32),
+                in_=h_half[j - (KINDS[j] == "a")][:].bitcast(F32)[:, :, cols, 0].rearrange("p u n -> p n u"),
+            )
+
+        def quantize_h(j):
+            h_codes[j] = work.tile([P, PAIR], U32, name="h_codes", align_bytes=64, bufs=3)
+            h_plane[j] = work.tile([P, PAIR], U8, name="h_plane", align_bytes=64, bufs=3)
+            nc.vector.quantize_mx(
+                out=h_codes[j][:].bitcast(FP8X4),
+                scales=h_plane[j][:],
+                in_=h_quad[j][:].rearrange("p n t -> p (n t)"),
+            )
+
+        def stage_two(j):
+            d = j // PAIRS
+            cov[j] = []
+            for a in range(2):
+                for half in range(R // BANK):
+                    bank = psum.tile([P, BANK], F32, name="cov", tag="cov", bufs=4)
+                    nc.tensor.matmul_mx(
+                        out=bank[:],
+                        lhsT=h_codes[j][:, a * P : (a + 1) * P].bitcast(FP8X4),
+                        lhsT_scale=h_plane[j][:, a * P : (a + 1) * P],
+                        rhs=v_raw[d][:, 2 * BANK * half : 2 * BANK * (half + 1)].bitcast(FP4X4),
+                        rhs_scale=vs[:, d, BANK * half : BANK * (half + 1)],
+                        start=True,
+                        stop=True,
+                    )
+                    cov[j].append(bank)
+
+        def normalise(j, then):
+            d, i = divmod(j, PAIRS)
+            for a in range(2):
+                tile_index = 2 * i + a
+                result = work.tile([P, R], F32, name="result", bufs=10)
+                for half in range(R // BANK):
+                    cols = slice(BANK * half, BANK * (half + 1))
+                    nc.vector.scalar_tensor_tensor(
+                        out=result[:, cols],
+                        in0=cov[j][2 * a + half][:],
+                        scalar=isp[:, d, tile_index : tile_index + 1],
+                        in1=isr[d][:, cols],
+                        op0=MULT,
+                        op1=MULT,
+                    )
+                    for q in then:
+                        if HQ_AFTER[q] == 2 * a + half + 1:
+                            quantize_h(q)
+                    if j == STEPS - 1:
+                        nc.sync.dma_start(out=out_hbm[d, :, tile_index, cols], in_=result[:, cols])
+                if j != STEPS - 1:
+                    nc.sync.dma_start(out=out_hbm[d, :, tile_index, :], in_=result[:])
+
+        sort_u(0)
+        sort_plane(0)
+        for k in range(-2, STEPS + 3):
+            ts = [j for j in range(STEPS) if T_STEP[j] == k]
+            js = [j for j in range(STEPS) if J_STEP[j] == k]
+            s2 = [j for j in range(STEPS) if S2_STEP[j] == k]
+            late = k in CFG.get("late", [])
+            for j in ts:
+                if not late:
+                    turn_probes(j)
+            for d in range(G):
+                if CFG.get("isr", [-1, 2, 5, 8])[d] == k:
+                    spread_isr(d)
+            if 0 <= k < STEPS:
+                stage_one(k)
+            if late:
+                scale_amplitudes(k)
+                for j in js:
+                    join_halves(j)
+                for j in ts:
+                    turn_probes(j)
+                for j in js:
+                    quantize_h(j)
+                js = []
+            for j in s2[:1]:
+                stage_two(j)
+            for j in ts:
+                quantize_probes(j)
+            for d in range(G):
+                if SORT_STEP[d] == k:
+                    sort_u(d)
+                if PLANE_STEP[d] == k:
+                    sort_plane(d)
+            if 0 <= k < STEPS and not late:
+                scale_amplitudes(k)
+            for j in js:
+                join_halves(j)
+            if not s2:
+                for j in js:
+                    quantize_h(j)
+            for n, j in enumerate(s2):
+                if n > 0:
+                    stage_two(j)
+                normalise(j, js if n == 0 else [])

@@ -3,7 +3,7 @@ from contextlib import ExitStack
 import concourse.mybir as mybir
 from concourse.masks import make_identity
 
-CFG = {"hq":[3,3,3,3,3,3,3,3,3,2,2,2],"kinds":"BAaAaBAaBAaB","loads":"lam x0 x1 U0 us0 P1 isr P2 gvs gusr V0 U1 isp P3 U2 P4 U3 P5 V1 P6 P7 P8 V2 P9 P10 P11 V3","j":[0,2,3,4,5,6,7,8,9,10,11,12],"s2":[1,3,4,5,6,7,8,9,10,11,12,13],"sort":[-9,-1,0,2],"plane":[-9,1,2,5],"late":[0]}
+CFG = {"chunks":[2,4,4,2,4,2,4,2],"loads":"x0 x1 us0 P1 U0 lam U1 P2 usR P3 P4 V0 vs0 isp isr0 U2 P5 U3 P6 V1 vsR isrR P7 P8 V2 P9 P10 P11 V3","seq":"U0 T0 T1 T2 T3 x0.0 T4 T5 x0.1 T6 T7 x1.0 x1.1 U1 T8 T9 x1.2 x1.3 c0 c1 T10 T11 x2.0 x2.1 c2 c3 T12 T13 x2.2 x2.3 c4 c5 U2 T14 T15 x3.0 x3.1 c6 c7 T16 T17 x4.0 x4.1 c8 c9 T18 T19 x4.2 x4.3 c10 c11 U3 T20 T21 x5.0 x5.1 c12 c13 T22 T23 x6.0 x6.1 c14 c15 x6.2 x6.3 c16 c17 x7.0 x7.1 c18 c19 c20 c21 c22 c23"}
 G, S, R, M = 4, 768, 1024, 512
 FLOPS = 2 * 2 * G * S * R * M
 
@@ -21,17 +21,12 @@ P = 128
 PACK = 4
 BANK = 512
 TILES = S // P
-PAIRS = TILES // 2
-PAIR = 2 * P
 PASSES = R // (P * PACK)
-STEPS = G * PAIRS
-KINDS = CFG.get("kinds", "AaB" * 4)
-T_STEP = CFG.get("t", [j - 2 for j in range(STEPS)])
-J_STEP = CFG.get("j", [j + 1 for j in range(STEPS)])
-S2_STEP = CFG.get("s2", [j + 2 for j in range(STEPS)])
-SORT_STEP = CFG.get("sort", [-9, -1, 0, 1])
-PLANE_STEP = CFG.get("plane", [-9, 1, 2, 3])
-HQ_AFTER = CFG.get("hq", [4] * STEPS)
+CHUNKS = CFG["chunks"]
+FIRST = [sum(CHUNKS[:c]) for c in range(len(CHUNKS))]
+CHUNK_OF = [c for c in range(len(CHUNKS)) for i in range(CHUNKS[c])]
+NB = CFG.get("nb", [2, 2, 4])
+PIN = {mybir.EngineType.PE, mybir.EngineType.SP, mybir.EngineType.Pool}
 
 
 def tile_elastic_mode_correlation_s14_kernel(
@@ -42,7 +37,7 @@ def tile_elastic_mode_correlation_s14_kernel(
         keep = ctx.enter_context(tc.tile_pool(name="keep", bufs=1))
         work = ctx.enter_context(tc.tile_pool(name="work", bufs=2))
         psum = ctx.enter_context(tc.psum_pool(name="psum", bufs=2))
-        ctx.enter_context(tc.manual_schedule())
+        ctx.enter_context(tc.manual_schedule(engines=PIN))
 
         def kept(shape, dtype, name):
             return keep.tile(shape, dtype, name=name, align_bytes=64)
@@ -52,8 +47,9 @@ def tile_elastic_mode_correlation_s14_kernel(
 
         us_first = kept([P, PASSES, M], U8, "us_first")
         us_rest = kept([P, (G - 1) * PASSES, M], U8, "us_rest")
-        vs = kept([P, G, R], U8, "vs")
-        for plane in (us_first, vs, us_rest):
+        vs_first = kept([P, 1, R], U8, "vs_first")
+        vs_rest = kept([P, G - 1, R], U8, "vs_rest")
+        for plane in (us_first, vs_first, us_rest, vs_rest):
             nc.vector.memset(plane[:].bitcast(I32), 0)
 
         def load_scale_rows(queue, plane, rows):
@@ -65,263 +61,184 @@ def tile_elastic_mode_correlation_s14_kernel(
 
         u_raw = [kept([P, PASSES, 2 * M], U8, "u_raw%d" % d) for d in range(G)]
         v_raw = [kept([P, 2 * R], U8, "v_raw%d" % d) for d in range(G)]
-        x_rows = [kept([P, R], BF16, "x%d" % i) for i in range(2)]
-        x_pair = [None] + [kept([P, 2, R], BF16, "xp%d" % j) for j in range(1, STEPS)]
+        x_rows = {}
         lam_bf = kept([P, G, PACK], BF16, "lam_bf")
         lam = kept([P, G, PACK], F32, "lam")
         isp = kept([P, G, TILES], BF16, "isp")
-        isr_rows = kept([P, G, R // P], BF16, "isr_rows")
+        isr_first = kept([P, R], BF16, "isr_first")
+        isr_rest = kept([P, (G - 1) * R], BF16, "isr_rest")
 
         x_hbm = probes.rearrange("d (p j) r -> d p j r", j=TILES)
         out_hbm = out.rearrange("d (p j) r -> d p j r", j=TILES)
 
-        def load_u(d):
-            nc.sync.dma_start(
-                out=u_raw[d][:].bitcast(I32),
-                in_=u_words.bitcast(I32)[PASSES * d : PASSES * (d + 1)].rearrange("g p n -> p g n"),
-            )
-
-        def load_v(d):
-            nc.sync.dma_start(out=v_raw[d][:].bitcast(I32), in_=v_words.bitcast(I32)[d])
-
-        def load_pair(j):
-            d, i = divmod(j, PAIRS)
-            nc.sync.dma_start(out=x_pair[j][:], in_=x_hbm[d, :, 2 * i : 2 * i + 2, :])
-
-        def small(name):
+        def load(name):
+            queue = nc.sync
+            if name[0] == "s":
+                queue = nc.scalar
+                name = name[1:]
             if name == "lam":
-                nc.sync.dma_start(out=lam_bf[:], in_=inv_lam.rearrange("d (p t) -> p d t", t=PACK))
-            if name == "isr":
-                nc.sync.dma_start(out=isr_rows[:], in_=inv_sd_res.rearrange("d (p c) -> p d c", p=P))
+                queue.dma_start(out=lam_bf[:], in_=inv_lam.rearrange("d (p t) -> p d t", t=PACK))
             if name == "isp":
-                nc.sync.dma_start(out=isp[:], in_=inv_sd_probe.rearrange("d (p j) -> p d j", j=TILES))
+                queue.dma_start(out=isp[:], in_=inv_sd_probe.rearrange("d (p j) -> p d j", j=TILES))
+            if name == "isr0":
+                queue.dma_start(out=isr_first[:], in_=inv_sd_res[0].partition_broadcast(P))
+            if name == "isrR":
+                queue.dma_start(out=isr_rest[:], in_=inv_sd_res[1:G].rearrange("d r -> (d r)").partition_broadcast(P))
             if name == "us0":
-                load_scale_rows(nc.sync, us_first, u_scales[0:PASSES])
-            if name == "usr":
-                load_scale_rows(nc.sync, us_rest, u_scales[PASSES:])
-            if name == "vs":
-                load_scale_rows(nc.sync, vs, v_scales)
-            if name == "gusr":
-                load_scale_rows(nc.gpsimd, us_rest, u_scales[PASSES:])
-            if name == "gvs":
-                load_scale_rows(nc.gpsimd, vs, v_scales)
-            if name == "gus0":
-                load_scale_rows(nc.gpsimd, us_first, u_scales[0:PASSES])
-            if name[0] == "x":
-                a = int(name[1:])
-                nc.sync.dma_start(out=x_rows[a][:], in_=x_hbm[0, :, a, :])
-            if name[0] == "P":
-                load_pair(int(name[1:]))
+                load_scale_rows(queue, us_first, u_scales[0:PASSES])
+            if name == "usR":
+                load_scale_rows(queue, us_rest, u_scales[PASSES:])
+            if name == "vs0":
+                load_scale_rows(queue, vs_first, v_scales[0:1])
+            if name == "vsR":
+                load_scale_rows(queue, vs_rest, v_scales[1:G])
+            if name[0] in "xP":
+                count = 1 if name[0] == "x" else 2
+                first = count * int(name[1:])
+                d, j = divmod(first, TILES)
+                rows = kept([P, count, R], BF16, name)
+                queue.dma_start(out=rows[:], in_=x_hbm[d, :, j : j + count, :])
+                for a in range(count):
+                    x_rows[first + a] = rows[:, a, :]
             if name[0] == "U":
-                load_u(int(name[1:]))
+                d = int(name[1:])
+                queue.dma_start(
+                    out=u_raw[d][:].bitcast(I32),
+                    in_=u_words.bitcast(I32)[PASSES * d : PASSES * (d + 1)].rearrange("g p n -> p g n"),
+                )
             if name[0] == "V":
-                load_v(int(name[1:]))
+                d = int(name[1:])
+                queue.dma_start(out=v_raw[d][:].bitcast(I32), in_=v_words.bitcast(I32)[d])
 
-        for name in CFG.get("loads", "isr x0 x1 U0 us0 lam P1 gvs gusr P2 U1 V0 isp P3 U2 P4 U3 P5 V1 P6 P7 P8 V2 P9 P10 P11 V3").split():
-            small(name)
+        for name in CFG["loads"].split():
+            load(name)
 
         nc.scalar.activation(out=lam[:], in_=lam_bf[:], func=COPY)
 
-        u_codes = [kept([P, PASSES, PACK, 2 * P], U8, "u_codes%d" % d) for d in range(G)]
+        u_codes = [[kept([P, PACK, 2 * P], U8, "u_codes%d_%d" % (d, g)) for g in range(PASSES)] for d in range(G)]
         u_plane = [kept([P, PASSES, PACK, P], U8, "u_plane%d" % d) for d in range(G)]
-        isr = [kept([P, R], BF16, "isr%d" % d) for d in range(G)]
 
         def sort_u(d):
-            nc.vector.tensor_copy(
-                out=u_codes[d][:].rearrange("p g t (m b) -> p g t m b", b=2),
-                in_=u_raw[d][:].rearrange("p g (m t b) -> p g t m b", t=PACK, b=2),
-            )
-
-        def sort_plane(d):
+            for g in range(PASSES):
+                nc.vector.tensor_copy(
+                    out=u_codes[d][g][:].rearrange("p t (m b) -> p t m b", b=2),
+                    in_=u_raw[d][:, g].rearrange("p (m t b) -> p t m b", t=PACK, b=2),
+                )
             rows = us_first[:] if d == 0 else us_rest[:, PASSES * (d - 1) : PASSES * d, :]
             nc.vector.tensor_copy(out=u_plane[d][:], in_=rows.rearrange("p g (m t) -> p g t m", t=PACK))
 
-        def spread_isr(d):
-            bank = psum.tile([P, BANK], F32, name="spread", tag="cov", bufs=4)
-            words = isr_rows[:].bitcast(F32)
-            for c in range(4):
-                nc.tensor.transpose(
-                    bank[:, c * P : (c + 1) * P], words[:, d, c : c + 1].to_broadcast([P, P]), ident[:]
-                )
+        x_codes, x_plane, h_half, h_codes, h_plane = {}, {}, {}, {}, {}
+
+        def turn_probes(i):
+            c = CHUNK_OF[i]
+            if i == FIRST[c]:
+                x_codes[c] = work.tile([P, PASSES, BANK], U32, name="x_codes", align_bytes=64, bufs=3)
+                x_plane[c] = work.tile([P, PASSES, BANK], U8, name="x_plane", align_bytes=64, bufs=3)
+            words = x_rows[i].bitcast(F32)
+            if i in CFG.get("presort", []):
+                sorted_words = work.tile([P, PASSES, 2, P], F32, name="sorted_words", bufs=3)
+                nc.vector.tensor_copy(out=sorted_words[:], in_=words.rearrange("p (g w u) -> p g u w", g=PASSES, u=2))
+            x_quad = work.tile([P, PASSES, P, PACK], BF16, name="x_quad", align_bytes=64, bufs=4)
+            bank = psum.tile([P, BANK], F32, name="turned", tag="turned", bufs=NB[0])
+            for g in range(PASSES):
+                for u in range(2):
+                    q = 2 * g + u
+                    src = words[:, 256 * g + u : 256 * (g + 1) : 2]
+                    if i in CFG.get("presort", []):
+                        src = sorted_words[:, g, u, :]
+                    nc.tensor.transpose(bank[:, q * P : (q + 1) * P], src, ident[:])
             nc.scalar.copy(
-                out=isr[d][:].bitcast(F32).rearrange("p (q c) -> p q c", c=4),
-                in_=bank[:].rearrange("p (c q) -> p q c", c=4),
+                out=x_quad[:].bitcast(F32),
+                in_=bank[:].rearrange("p (g u r) -> p g r u", g=PASSES, u=2),
             )
-
-        x_quad, x_codes, x_plane, amp, h_half, h_quad, h_codes, h_plane, cov = {}, {}, {}, {}, {}, {}, {}, {}, {}
-
-        def turn_probes(j):
-            x_quad[j] = work.tile([P, PASSES, PAIR, PACK], BF16, name="x_quad", align_bytes=64, bufs=3)
-            for a in range(2):
-                rows = x_rows[a][:] if j == 0 else x_pair[j][:, a, :]
-                words = rows.bitcast(F32)
-                bank = psum.tile([P, BANK], F32, name="turned", tag="turned")
-                for g in range(PASSES):
-                    for u in range(2):
-                        c = 2 * g + u
-                        nc.tensor.transpose(
-                            bank[:, c * P : (c + 1) * P], words[:, 256 * g + u : 256 * (g + 1) : 2], ident[:]
-                        )
-                nc.scalar.copy(
-                    out=x_quad[j][:].bitcast(F32)[:, :, a * P : (a + 1) * P, :],
-                    in_=bank[:].rearrange("p (g u r) -> p g r u", g=PASSES, u=2),
-                )
-
-        def quantize_probes(j):
-            d, i = divmod(j, PAIRS)
-            chunk = j - (KINDS[j] == "a")
-            if KINDS[j] != "a":
-                x_codes[chunk] = work.tile([P, PASSES, BANK], U32, name="x_codes", align_bytes=64, bufs=3)
-                x_plane[chunk] = work.tile([P, PASSES, BANK], U8, name="x_plane", align_bytes=64, bufs=3)
-            cols = slice(PAIR, 2 * PAIR) if KINDS[j] == "a" else slice(0, PAIR)
+            cols = slice((i - FIRST[c]) * P, (i - FIRST[c] + 1) * P)
             for g in range(PASSES):
                 nc.vector.quantize_mx(
-                    out=x_codes[chunk][:, g, cols].bitcast(FP8X4),
-                    scales=x_plane[chunk][:, g, cols],
-                    in_=x_quad[j][:, g].rearrange("p n t -> p (n t)"),
+                    out=x_codes[c][:, g, cols].bitcast(FP8X4),
+                    scales=x_plane[c][:, g, cols],
+                    in_=x_quad[:, g].rearrange("p n t -> p (n t)"),
                 )
 
-        def project(bank_cols, d, t, chunk, cols):
-            for g in range(PASSES):
-                nc.tensor.matmul_mx(
-                    out=bank_cols,
-                    lhsT=u_codes[d][:, g, t, :].bitcast(FP4X4),
-                    lhsT_scale=u_plane[d][:, g, t, :],
-                    rhs=x_codes[chunk][:, g, cols].bitcast(FP8X4),
-                    rhs_scale=x_plane[chunk][:, g, cols],
-                    start=(g == 0),
-                    stop=(g == PASSES - 1),
-                )
-
-        def stage_one(j):
-            d, i = divmod(j, PAIRS)
-            chunk = j - (KINDS[j] == "a")
-            amp[j] = []
-            for b in range(2):
-                bank = psum.tile([P, BANK], F32, name="amp", tag="amp")
-                if KINDS[j] != "B":
-                    i = int(KINDS[j] == "a")
-                    project(bank[:], d, 2 * b + i, chunk, slice(0, BANK))
-                    amp[j].append((2 * b + i, bank[:], BANK))
-                else:
-                    for e in range(2):
-                        for a in range(2):
-                            c = 2 * e + a
-                            project(bank[:, c * P : (c + 1) * P], d, 2 * e + b, chunk, slice(a * P, (a + 1) * P))
-                        amp[j].append((2 * e + b, bank[:, e * PAIR : (e + 1) * PAIR], PAIR))
-
-        def scale_amplitudes(j):
-            d, i = divmod(j, PAIRS)
-            chunk = j - (KINDS[j] == "a")
-            if KINDS[j] != "a":
-                h_half[chunk] = work.tile([P, 2, BANK, 2], BF16, name="h_half", bufs=3)
-            for t, bank_cols, width in amp[j]:
+        def stage_one(c, b):
+            size = CHUNKS[c]
+            d = FIRST[c] // TILES
+            width = size * P
+            if b == 0:
+                h_half[c] = work.tile([P, 2, BANK, 2], BF16, name="h_half", bufs=3)
+            bank = psum.tile([P, BANK], F32, name="amp", tag="amp", bufs=NB[1])
+            slots = (0, 2, 1, 3)[b * PACK // size : (b + 1) * PACK // size]
+            step = BANK if size == PACK else P
+            for n, t in enumerate(slots):
+                for c0 in range(0, width, step):
+                    for g in range(PASSES):
+                        nc.tensor.matmul_mx(
+                            out=bank[:, n * width + c0 : n * width + c0 + step],
+                            lhsT=u_codes[d][g][:, t, :].bitcast(FP4X4),
+                            lhsT_scale=u_plane[d][:, g, t, :],
+                            rhs=x_codes[c][:, g, c0 : c0 + step].bitcast(FP8X4),
+                            rhs_scale=x_plane[c][:, g, c0 : c0 + step],
+                            start=(g == 0),
+                            stop=(g == PASSES - 1),
+                        )
+            for n, t in enumerate(slots):
                 nc.scalar.activation(
-                    out=h_half[chunk][:, t // 2, 0:width, t % 2],
-                    in_=bank_cols,
+                    out=h_half[c][:, t // 2, 0:width, t % 2],
+                    in_=bank[:, n * width : (n + 1) * width],
                     func=COPY,
                     scale=lam[:, d, t : t + 1],
                 )
-
-        def join_halves(j):
-            d, i = divmod(j, PAIRS)
-            cols = slice(PAIR, 2 * PAIR) if KINDS[j] == "a" else slice(0, PAIR)
-            h_quad[j] = work.tile([P, PAIR, PACK], BF16, name="h_quad", align_bytes=64, bufs=3)
-            nc.scalar.copy(
-                out=h_quad[j][:].bitcast(F32),
-                in_=h_half[j - (KINDS[j] == "a")][:].bitcast(F32)[:, :, cols, 0].rearrange("p u n -> p n u"),
-            )
-
-        def quantize_h(j):
-            h_codes[j] = work.tile([P, PAIR], U32, name="h_codes", align_bytes=64, bufs=3)
-            h_plane[j] = work.tile([P, PAIR], U8, name="h_plane", align_bytes=64, bufs=3)
-            nc.vector.quantize_mx(
-                out=h_codes[j][:].bitcast(FP8X4),
-                scales=h_plane[j][:],
-                in_=h_quad[j][:].rearrange("p n t -> p (n t)"),
-            )
-
-        def stage_two(j):
-            d = j // PAIRS
-            cov[j] = []
-            for a in range(2):
-                for half in range(R // BANK):
-                    bank = psum.tile([P, BANK], F32, name="cov", tag="cov", bufs=4)
-                    nc.tensor.matmul_mx(
-                        out=bank[:],
-                        lhsT=h_codes[j][:, a * P : (a + 1) * P].bitcast(FP8X4),
-                        lhsT_scale=h_plane[j][:, a * P : (a + 1) * P],
-                        rhs=v_raw[d][:, 2 * BANK * half : 2 * BANK * (half + 1)].bitcast(FP4X4),
-                        rhs_scale=vs[:, d, BANK * half : BANK * (half + 1)],
-                        start=True,
-                        stop=True,
+            if b == size - 1:
+                for i in range(FIRST[c], FIRST[c] + size):
+                    cols = slice((i - FIRST[c]) * P, (i - FIRST[c] + 1) * P)
+                    h_quad = work.tile([P, P, PACK], BF16, name="h_quad", align_bytes=64, bufs=6)
+                    src = h_half[c][:].bitcast(F32)[:, :, cols, 0].rearrange("p u n -> p n u")
+                    if i in CFG.get("vjoin", []):
+                        nc.vector.tensor_copy(out=h_quad[:].bitcast(F32), in_=src)
+                    else:
+                        nc.scalar.copy(out=h_quad[:].bitcast(F32), in_=src)
+                    h_codes[i] = work.tile([P, P], U32, name="h_codes", align_bytes=64, bufs=8)
+                    h_plane[i] = work.tile([P, P], U8, name="h_plane", align_bytes=64, bufs=8)
+                    nc.vector.quantize_mx(
+                        out=h_codes[i][:].bitcast(FP8X4),
+                        scales=h_plane[i][:],
+                        in_=h_quad[:].rearrange("p n t -> p (n t)"),
                     )
-                    cov[j].append(bank)
 
-        def normalise(j, then):
-            d, i = divmod(j, PAIRS)
-            for a in range(2):
-                tile_index = 2 * i + a
-                result = work.tile([P, R], F32, name="result", bufs=10)
-                for half in range(R // BANK):
-                    cols = slice(BANK * half, BANK * (half + 1))
-                    nc.vector.scalar_tensor_tensor(
-                        out=result[:, cols],
-                        in0=cov[j][2 * a + half][:],
-                        scalar=isp[:, d, tile_index : tile_index + 1],
-                        in1=isr[d][:, cols],
-                        op0=MULT,
-                        op1=MULT,
-                    )
-                    for q in then:
-                        if HQ_AFTER[q] == 2 * a + half + 1:
-                            quantize_h(q)
-                    if j == STEPS - 1:
-                        nc.sync.dma_start(out=out_hbm[d, :, tile_index, cols], in_=result[:, cols])
-                if j != STEPS - 1:
-                    nc.sync.dma_start(out=out_hbm[d, :, tile_index, :], in_=result[:])
+        def stage_two(i):
+            d, j = divmod(i, TILES)
+            result = work.tile([P, R], F32, name="result", bufs=10)
+            for half in range(R // BANK):
+                cols = slice(BANK * half, BANK * (half + 1))
+                bank = psum.tile([P, BANK], F32, name="cov", tag="cov", bufs=NB[2])
+                nc.tensor.matmul_mx(
+                    out=bank[:],
+                    lhsT=h_codes[i][:].bitcast(FP8X4),
+                    lhsT_scale=h_plane[i][:],
+                    rhs=v_raw[d][:, 2 * BANK * half : 2 * BANK * (half + 1)].bitcast(FP4X4),
+                    rhs_scale=vs_first[:, 0, cols] if d == 0 else vs_rest[:, d - 1, cols],
+                    start=True,
+                    stop=True,
+                )
+                nc.vector.scalar_tensor_tensor(
+                    out=result[:, cols],
+                    in0=bank[:],
+                    scalar=isp[:, d, j : j + 1],
+                    in1=isr_first[:, cols] if d == 0 else isr_rest[:, (d - 1) * R + BANK * half : (d - 1) * R + BANK * (half + 1)],
+                    op0=MULT,
+                    op1=MULT,
+                )
+                if i >= CFG.get("fine", 22):
+                    nc.sync.dma_start(out=out_hbm[d, :, j, cols], in_=result[:, cols])
+            if i < CFG.get("fine", 22):
+                nc.sync.dma_start(out=out_hbm[d, :, j, :], in_=result[:])
 
-        sort_u(0)
-        sort_plane(0)
-        for k in range(-2, STEPS + 3):
-            ts = [j for j in range(STEPS) if T_STEP[j] == k]
-            js = [j for j in range(STEPS) if J_STEP[j] == k]
-            s2 = [j for j in range(STEPS) if S2_STEP[j] == k]
-            late = k in CFG.get("late", [])
-            for j in ts:
-                if not late:
-                    turn_probes(j)
-            for d in range(G):
-                if CFG.get("isr", [-1, 2, 5, 8])[d] == k:
-                    spread_isr(d)
-            if 0 <= k < STEPS:
-                stage_one(k)
-            if late:
-                scale_amplitudes(k)
-                for j in js:
-                    join_halves(j)
-                for j in ts:
-                    turn_probes(j)
-                for j in js:
-                    quantize_h(j)
-                js = []
-            for j in s2[:1]:
+        for word in CFG["seq"].split():
+            kind, j, b = word[0], int(word[1:].split(".")[0]), int((word + ".0").split(".")[1])
+            if kind == "U":
+                sort_u(j)
+            if kind == "T":
+                turn_probes(j)
+            if kind == "x":
+                stage_one(j, b)
+            if kind == "c":
                 stage_two(j)
-            for j in ts:
-                quantize_probes(j)
-            for d in range(G):
-                if SORT_STEP[d] == k:
-                    sort_u(d)
-                if PLANE_STEP[d] == k:
-                    sort_plane(d)
-            if 0 <= k < STEPS and not late:
-                scale_amplitudes(k)
-            for j in js:
-                join_halves(j)
-            if not s2:
-                for j in js:
-                    quantize_h(j)
-            for n, j in enumerate(s2):
-                if n > 0:
-                    stage_two(j)
-                normalise(j, js if n == 0 else [])

@@ -3,7 +3,7 @@ from contextlib import ExitStack
 import concourse.mybir as mybir
 from concourse.masks import make_identity
 
-CFG = {"chunks":[2,4,4,2,4,2,4,2],"loads":"x0 x1 us0 P1 U0 lam U1 P2 usR P3 P4 V0 vs0 isp isr0 U2 P5 U3 P6 V1 vsR isrR P7 P8 V2 P9 P10 P11 V3","seq":"U0 T0 T1 T2 T3 x0.0 T4 T5 x0.1 T6 T7 x1.0 x1.1 U1 T8 T9 x1.2 x1.3 c0 c1 T10 T11 x2.0 x2.1 c2 c3 T12 T13 x2.2 x2.3 c4 c5 U2 T14 T15 x3.0 x3.1 c6 c7 T16 T17 x4.0 x4.1 c8 c9 T18 T19 x4.2 x4.3 c10 c11 U3 T20 T21 x5.0 x5.1 c12 c13 T22 T23 x6.0 x6.1 c14 c15 x6.2 x6.3 c16 c17 x7.0 x7.1 c18 c19 c20 c21 c22 c23"}
+CFG = {"chunks":[2,4,4,2,4,2,4,2],"loads":"x0 x1 us0 P1 U0 lam U1 P2 usR P3 P4 V0 vs0 isp isr0 U2 P5 U3 P6 V1 vsR isrR P7 P8 V2 P9 P10 P11 V3","seq":"U0 T0 T1 T2 T3 x0.0 T4 T5 x0.1 T6 T7 x1.0 x1.1 U1 T8 T9 x1.2 x1.3 c0 c1 T10 T11 x2.0 x2.1 c2 c3 T12 T13 x2.2 x2.3 c4 c5 U2 T14 T15 x3.0 x3.1 c6 c7 T16 T17 x4.0 x4.1 c8 c9 T18 T19 x4.2 x4.3 c10 c11 U3 T20 T21 x5.0 x5.1 c12 c13 T22 T23 x6.0 x6.1 c14 c15 x6.2 x6.3 c16 c17 x7.0 x7.1 c18 c19 c20 c21 c22 c23","vjoin":[0,1]}
 G, S, R, M = 4, 768, 1024, 512
 FLOPS = 2 * 2 * G * S * R * M
 
@@ -164,9 +164,9 @@ def tile_elastic_mode_correlation_s14_kernel(
             d = FIRST[c] // TILES
             width = size * P
             if b == 0:
-                h_half[c] = work.tile([P, 2, BANK, 2], BF16, name="h_half", bufs=3)
+                h_half[c] = work.tile([P, PACK, BANK], BF16, name="h_half", bufs=3)
             bank = psum.tile([P, BANK], F32, name="amp", tag="amp", bufs=NB[1])
-            slots = (0, 2, 1, 3)[b * PACK // size : (b + 1) * PACK // size]
+            slots = (0, 1, 2, 3)[b * PACK // size : (b + 1) * PACK // size]
             step = BANK if size == PACK else P
             for n, t in enumerate(slots):
                 for c0 in range(0, width, step):
@@ -182,7 +182,7 @@ def tile_elastic_mode_correlation_s14_kernel(
                         )
             for n, t in enumerate(slots):
                 nc.scalar.activation(
-                    out=h_half[c][:, t // 2, 0:width, t % 2],
+                    out=h_half[c][:, t, 0:width],
                     in_=bank[:, n * width : (n + 1) * width],
                     func=COPY,
                     scale=lam[:, d, t : t + 1],
@@ -191,11 +191,12 @@ def tile_elastic_mode_correlation_s14_kernel(
                 for i in range(FIRST[c], FIRST[c] + size):
                     cols = slice((i - FIRST[c]) * P, (i - FIRST[c] + 1) * P)
                     h_quad = work.tile([P, P, PACK], BF16, name="h_quad", align_bytes=64, bufs=6)
-                    src = h_half[c][:].bitcast(F32)[:, :, cols, 0].rearrange("p u n -> p n u")
+                    src = h_half[c][:, :, cols].rearrange("p t (c i) -> p c t i", i=4)
+                    dst = h_quad[:].rearrange("p (c i) t -> p c t i", i=4)
                     if i in CFG.get("vjoin", []):
-                        nc.vector.tensor_copy(out=h_quad[:].bitcast(F32), in_=src)
+                        nc.vector.tensor_copy(out=dst, in_=src)
                     else:
-                        nc.scalar.copy(out=h_quad[:].bitcast(F32), in_=src)
+                        nc.scalar.copy(out=dst, in_=src)
                     h_codes[i] = work.tile([P, P], U32, name="h_codes", align_bytes=64, bufs=8)
                     h_plane[i] = work.tile([P, P], U8, name="h_plane", align_bytes=64, bufs=8)
                     nc.vector.quantize_mx(

from contextlib import ExitStack

import concourse.mybir as mybir
from concourse.masks import make_identity

CFG = {"chunks":[2,4,4,2,4,2,4,2],"loads":"x0 x1 us0 P1 U0 lam U1 P2 usR P3 P4 V0 vs0 isp isr0 U2 P5 U3 P6 V1 vsR isrR P7 P8 V2 P9 P10 P11 V3","seq":"U0 T0 T1 T2 T3 x0.0 T4 T5 x0.1 T6 T7 x1.0 x1.1 U1 T8 T9 x1.2 x1.3 c0 c1 T10 T11 x2.0 x2.1 c2 c3 T12 T13 x2.2 x2.3 c4 c5 U2 T14 T15 x3.0 x3.1 c6 c7 T16 T17 x4.0 x4.1 c8 c9 T18 T19 x4.2 x4.3 c10 c11 U3 T20 T21 x5.0 x5.1 c12 c13 T22 T23 x6.0 x6.1 c14 c15 x6.2 x6.3 c16 c17 x7.0 x7.1 c18 c19 c20 c21 c22 c23","vjoin":[0,1]}
G, S, R, M = 4, 768, 1024, 512
FLOPS = 2 * 2 * G * S * R * M

F32 = mybir.dt.float32
BF16 = mybir.dt.bfloat16
I32 = mybir.dt.int32
U32 = mybir.dt.uint32
U8 = mybir.dt.uint8
FP8X4 = mybir.dt.float8_e4m3fn_x4
FP4X4 = mybir.dt.float4_e2m1fn_x4
COPY = mybir.ActivationFunctionType.Copy
MULT = mybir.AluOpType.mult

P = 128
PACK = 4
BANK = 512
TILES = S // P
PASSES = R // (P * PACK)
CHUNKS = CFG["chunks"]
FIRST = [sum(CHUNKS[:c]) for c in range(len(CHUNKS))]
CHUNK_OF = [c for c in range(len(CHUNKS)) for i in range(CHUNKS[c])]
NB = CFG.get("nb", [2, 2, 4])
PIN = {mybir.EngineType.PE, mybir.EngineType.SP, mybir.EngineType.Pool}


def tile_elastic_mode_correlation_s14_kernel(
    tc, probes, u_words, u_scales, inv_lam, v_words, v_scales, inv_sd_probe, inv_sd_res, out
):
    nc = tc.nc
    with ExitStack() as ctx:
        keep = ctx.enter_context(tc.tile_pool(name="keep", bufs=1))
        work = ctx.enter_context(tc.tile_pool(name="work", bufs=2))
        psum = ctx.enter_context(tc.psum_pool(name="psum", bufs=2))
        ctx.enter_context(tc.manual_schedule(engines=PIN))

        def kept(shape, dtype, name):
            return keep.tile(shape, dtype, name=name, align_bytes=64)

        ident = kept([P, P], F32, "ident")
        make_identity(nc, ident[:])

        us_first = kept([P, PASSES, M], U8, "us_first")
        us_rest = kept([P, (G - 1) * PASSES, M], U8, "us_rest")
        vs_first = kept([P, 1, R], U8, "vs_first")
        vs_rest = kept([P, G - 1, R], U8, "vs_rest")
        for plane in (us_first, vs_first, us_rest, vs_rest):
            nc.vector.memset(plane[:].bitcast(I32), 0)

        def load_scale_rows(queue, plane, rows):
            for r in range(4):
                queue.dma_start(
                    out=plane[:].bitcast(I32)[r:P:32],
                    in_=rows.bitcast(I32)[:, r:16:4, :].rearrange("g q n -> q g n"),
                )

        u_raw = [kept([P, PASSES, 2 * M], U8, "u_raw%d" % d) for d in range(G)]
        v_raw = [kept([P, 2 * R], U8, "v_raw%d" % d) for d in range(G)]
        x_rows = {}
        lam_bf = kept([P, G, PACK], BF16, "lam_bf")
        lam = kept([P, G, PACK], F32, "lam")
        isp = kept([P, G, TILES], BF16, "isp")
        isr_first = kept([P, R], BF16, "isr_first")
        isr_rest = kept([P, (G - 1) * R], BF16, "isr_rest")

        x_hbm = probes.rearrange("d (p j) r -> d p j r", j=TILES)
        out_hbm = out.rearrange("d (p j) r -> d p j r", j=TILES)

        def load(name):
            queue = nc.sync
            if name[0] == "s":
                queue = nc.scalar
                name = name[1:]
            if name == "lam":
                queue.dma_start(out=lam_bf[:], in_=inv_lam.rearrange("d (p t) -> p d t", t=PACK))
            if name == "isp":
                queue.dma_start(out=isp[:], in_=inv_sd_probe.rearrange("d (p j) -> p d j", j=TILES))
            if name == "isr0":
                queue.dma_start(out=isr_first[:], in_=inv_sd_res[0].partition_broadcast(P))
            if name == "isrR":
                queue.dma_start(out=isr_rest[:], in_=inv_sd_res[1:G].rearrange("d r -> (d r)").partition_broadcast(P))
            if name == "us0":
                load_scale_rows(queue, us_first, u_scales[0:PASSES])
            if name == "usR":
                load_scale_rows(queue, us_rest, u_scales[PASSES:])
            if name == "vs0":
                load_scale_rows(queue, vs_first, v_scales[0:1])
            if name == "vsR":
                load_scale_rows(queue, vs_rest, v_scales[1:G])
            if name[0] in "xP":
                count = 1 if name[0] == "x" else 2
                first = count * int(name[1:])
                d, j = divmod(first, TILES)
                rows = kept([P, count, R], BF16, name)
                queue.dma_start(out=rows[:], in_=x_hbm[d, :, j : j + count, :])
                for a in range(count):
                    x_rows[first + a] = rows[:, a, :]
            if name[0] == "U":
                d = int(name[1:])
                queue.dma_start(
                    out=u_raw[d][:].bitcast(I32),
                    in_=u_words.bitcast(I32)[PASSES * d : PASSES * (d + 1)].rearrange("g p n -> p g n"),
                )
            if name[0] == "V":
                d = int(name[1:])
                queue.dma_start(out=v_raw[d][:].bitcast(I32), in_=v_words.bitcast(I32)[d])

        for name in CFG["loads"].split():
            load(name)

        nc.scalar.activation(out=lam[:], in_=lam_bf[:], func=COPY)

        u_codes = [[kept([P, PACK, 2 * P], U8, "u_codes%d_%d" % (d, g)) for g in range(PASSES)] for d in range(G)]
        u_plane = [kept([P, PASSES, PACK, P], U8, "u_plane%d" % d) for d in range(G)]

        def sort_u(d):
            for g in range(PASSES):
                nc.vector.tensor_copy(
                    out=u_codes[d][g][:].rearrange("p t (m b) -> p t m b", b=2),
                    in_=u_raw[d][:, g].rearrange("p (m t b) -> p t m b", t=PACK, b=2),
                )
            rows = us_first[:] if d == 0 else us_rest[:, PASSES * (d - 1) : PASSES * d, :]
            nc.vector.tensor_copy(out=u_plane[d][:], in_=rows.rearrange("p g (m t) -> p g t m", t=PACK))

        x_codes, x_plane, h_half, h_codes, h_plane = {}, {}, {}, {}, {}

        def turn_probes(i):
            c = CHUNK_OF[i]
            if i == FIRST[c]:
                x_codes[c] = work.tile([P, PASSES, BANK], U32, name="x_codes", align_bytes=64, bufs=3)
                x_plane[c] = work.tile([P, PASSES, BANK], U8, name="x_plane", align_bytes=64, bufs=3)
            words = x_rows[i].bitcast(F32)
            if i in CFG.get("presort", []):
                sorted_words = work.tile([P, PASSES, 2, P], F32, name="sorted_words", bufs=3)
                nc.vector.tensor_copy(out=sorted_words[:], in_=words.rearrange("p (g w u) -> p g u w", g=PASSES, u=2))
            x_quad = work.tile([P, PASSES, P, PACK], BF16, name="x_quad", align_bytes=64, bufs=4)
            bank = psum.tile([P, BANK], F32, name="turned", tag="turned", bufs=NB[0])
            for g in range(PASSES):
                for u in range(2):
                    q = 2 * g + u
                    src = words[:, 256 * g + u : 256 * (g + 1) : 2]
                    if i in CFG.get("presort", []):
                        src = sorted_words[:, g, u, :]
                    nc.tensor.transpose(bank[:, q * P : (q + 1) * P], src, ident[:])
            nc.scalar.copy(
                out=x_quad[:].bitcast(F32),
                in_=bank[:].rearrange("p (g u r) -> p g r u", g=PASSES, u=2),
            )
            cols = slice((i - FIRST[c]) * P, (i - FIRST[c] + 1) * P)
            for g in range(PASSES):
                nc.vector.quantize_mx(
                    out=x_codes[c][:, g, cols].bitcast(FP8X4),
                    scales=x_plane[c][:, g, cols],
                    in_=x_quad[:, g].rearrange("p n t -> p (n t)"),
                )

        def stage_one(c, b):
            size = CHUNKS[c]
            d = FIRST[c] // TILES
            width = size * P
            if b == 0:
                h_half[c] = work.tile([P, PACK, BANK], BF16, name="h_half", bufs=3)
            bank = psum.tile([P, BANK], F32, name="amp", tag="amp", bufs=NB[1])
            slots = (0, 1, 2, 3)[b * PACK // size : (b + 1) * PACK // size]
            step = BANK if size == PACK else P
            for n, t in enumerate(slots):
                for c0 in range(0, width, step):
                    for g in range(PASSES):
                        nc.tensor.matmul_mx(
                            out=bank[:, n * width + c0 : n * width + c0 + step],
                            lhsT=u_codes[d][g][:, t, :].bitcast(FP4X4),
                            lhsT_scale=u_plane[d][:, g, t, :],
                            rhs=x_codes[c][:, g, c0 : c0 + step].bitcast(FP8X4),
                            rhs_scale=x_plane[c][:, g, c0 : c0 + step],
                            start=(g == 0),
                            stop=(g == PASSES - 1),
                        )
            for n, t in enumerate(slots):
                nc.scalar.activation(
                    out=h_half[c][:, t, 0:width],
                    in_=bank[:, n * width : (n + 1) * width],
                    func=COPY,
                    scale=lam[:, d, t : t + 1],
                )
            if b == size - 1:
                for i in range(FIRST[c], FIRST[c] + size):
                    cols = slice((i - FIRST[c]) * P, (i - FIRST[c] + 1) * P)
                    h_quad = work.tile([P, P, PACK], BF16, name="h_quad", align_bytes=64, bufs=6)
                    src = h_half[c][:, :, cols].rearrange("p t (c i) -> p c t i", i=4)
                    dst = h_quad[:].rearrange("p (c i) t -> p c t i", i=4)
                    if i in CFG.get("vjoin", []):
                        nc.vector.tensor_copy(out=dst, in_=src)
                    else:
                        nc.scalar.copy(out=dst, in_=src)
                    h_codes[i] = work.tile([P, P], U32, name="h_codes", align_bytes=64, bufs=8)
                    h_plane[i] = work.tile([P, P], U8, name="h_plane", align_bytes=64, bufs=8)
                    nc.vector.quantize_mx(
                        out=h_codes[i][:].bitcast(FP8X4),
                        scales=h_plane[i][:],
                        in_=h_quad[:].rearrange("p n t -> p (n t)"),
                    )

        def stage_two(i):
            d, j = divmod(i, TILES)
            result = work.tile([P, R], F32, name="result", bufs=10)
            for half in range(R // BANK):
                cols = slice(BANK * half, BANK * (half + 1))
                bank = psum.tile([P, BANK], F32, name="cov", tag="cov", bufs=NB[2])
                nc.tensor.matmul_mx(
                    out=bank[:],
                    lhsT=h_codes[i][:].bitcast(FP8X4),
                    lhsT_scale=h_plane[i][:],
                    rhs=v_raw[d][:, 2 * BANK * half : 2 * BANK * (half + 1)].bitcast(FP4X4),
                    rhs_scale=vs_first[:, 0, cols] if d == 0 else vs_rest[:, d - 1, cols],
                    start=True,
                    stop=True,
                )
                nc.vector.scalar_tensor_tensor(
                    out=result[:, cols],
                    in0=bank[:],
                    scalar=isp[:, d, j : j + 1],
                    in1=isr_first[:, cols] if d == 0 else isr_rest[:, (d - 1) * R + BANK * half : (d - 1) * R + BANK * (half + 1)],
                    op0=MULT,
                    op1=MULT,
                )
                if i >= CFG.get("fine", 22):
                    nc.sync.dma_start(out=out_hbm[d, :, j, cols], in_=result[:, cols])
            if i < CFG.get("fine", 22):
                nc.sync.dma_start(out=out_hbm[d, :, j, :], in_=result[:])

        for word in CFG["seq"].split():
            kind, j, b = word[0], int(word[1:].split(".")[0]), int((word + ".0").split(".")[1])
            if kind == "U":
                sort_u(j)
            if kind == "T":
                turn_probes(j)
            if kind == "x":
                stage_one(j, b)
            if kind == "c":
                stage_two(j)
